import numpy as np
import ml_dtypes


def mxq(x, axis, fmt="e4m3"):
    dtype, down = {"e4m3": (ml_dtypes.float8_e4m3fn, 7), "e5m2": (ml_dtypes.float8_e5m2, 14)}[fmt]
    v = np.moveaxis(np.asarray(x, np.float32).astype(ml_dtypes.bfloat16).astype(np.float64), axis, -1)
    blocks = v.reshape(v.shape[:-1] + (-1, 32))
    amax = np.abs(blocks).max(-1, keepdims=True)
    byte = np.maximum(np.where(amax > 0, np.frexp(amax)[1] - 1 + 127, 0) - down, 1)
    scale = np.exp2(byte - 127.0)
    codes = (blocks / scale).astype(np.float32).astype(dtype).astype(np.float64)
    return np.moveaxis((codes * scale).reshape(v.shape), -1, axis)


WIDE = False


def mx_kscale(k):
    if not WIDE:
        return np.ones(k)
    levels = np.array([10, -10, 5, -5, 0])
    if k % 512:
        return np.exp2(np.random.permutation(np.resize(levels, k // 32))).repeat(32)
    a = np.empty((k // 512, 16))
    for p in range(k // 512):
        a[p, :8] = np.random.permutation(np.resize(levels, 8))
        for g in range(8):
            far = levels[np.abs(levels - a[p, g]) >= 10]
            a[p, g + 8] = far[np.random.randint(len(far))]
    return np.exp2(a.ravel()).repeat(32)


BF16 = ml_dtypes.bfloat16


def bf(x):
    return np.asarray(x, np.float32).astype(BF16)


def f64(x):
    return np.asarray(x).astype(np.float64)


E2M1 = np.array([0.0, 0.5, 1.0, 1.5, 2.0, 3.0, 4.0, 6.0, -0.0, -0.5, -1.0, -1.5, -2.0, -3.0, -4.0, -6.0])


def pack_weight(w, fmt):
    k, n = w.shape
    w = f64(bf(w)).reshape(k // 32, 32, n)
    amax = np.abs(w).max(1)
    if fmt == "e4m3":
        byte = np.frexp(amax)[1] - 1 + 127 - 7
    else:
        mant, ex = np.frexp(amax / 6.0)
        byte = np.where(mant > 0.5, ex, ex - 1) + 127
    byte = np.clip(np.where(amax > 0, byte, 1), 1, 254)
    scaled = (w * np.exp2(127.0 - byte)[:, None, :]).reshape(k, n).astype(np.float32)
    by_word = np.ascontiguousarray(scaled.reshape(k // 512, 128, 4, n).transpose(0, 1, 3, 2))
    if fmt == "e4m3":
        words = by_word.astype(ml_dtypes.float8_e4m3fn).view(np.uint8)
    else:
        c = by_word.astype(ml_dtypes.float4_e2m1fn).view(np.uint8) & 0xF
        words = c[..., 0::2] | (c[..., 1::2] << 4)
    return np.ascontiguousarray(words), np.ascontiguousarray(byte.astype(np.uint8).reshape(k // 512, 16, n))


def unpack_weight(words, scales, fmt):
    g, p, n, _ = words.shape
    if fmt == "e4m3":
        vals = np.ascontiguousarray(words).view(ml_dtypes.float8_e4m3fn).astype(np.float64)
    else:
        nib = np.empty((g, p, n, 4), np.uint8)
        nib[..., 0::2] = words & 0xF
        nib[..., 1::2] = words >> 4
        vals = E2M1[nib]
    vals = vals * np.repeat(np.exp2(scales.astype(np.float64) - 127.0), 8, axis=1)[..., None]
    return vals.transpose(0, 1, 3, 2).reshape(g * 512, n)

def planes(Y):
    n, m = Y.shape
    b = f64(bf(Y)).reshape(n // 32, 32, m)
    amax = np.abs(b).max(1)
    byte = np.clip(np.where(amax > 0, np.frexp(amax)[1] - 1 + 127 - 7, 1), 1, 254)
    codes = (b * np.exp2(127.0 - byte)[:, None, :]).reshape(n, m).astype(np.float32).astype(ml_dtypes.float8_e4m3fn).view(np.uint8)
    words = codes.reshape(n // 512, 128, 4, m).transpose(0, 1, 3, 2)
    return np.ascontiguousarray(words), np.ascontiguousarray(byte.astype(np.uint8).reshape(n // 512, 16, m))


B, N, D, A, L = 4, 512, 512, 512, 1024


def setup_inputs():
    s, t = mx_kscale(D), mx_kscale(A)
    h = bf(np.random.standard_normal((B, N, D)) * s)
    w_words, w_scales = pack_weight(np.random.standard_normal((D, A)) / np.sqrt(D) / s[:, None], "e4m3")
    g = bf((1.0 + 0.1 * np.random.standard_normal(A)) * t)
    u_words, u_scales = pack_weight((1.5 * np.random.standard_normal((L, A)) / np.sqrt(A) / t[None, :]).T, "e4m3")
    beta_words, beta_scales = pack_weight((np.random.standard_normal((L, D)) / np.sqrt(D) / s[None, :]).T, "e4m3")
    c = bf(0.3 * np.random.standard_normal(L))
    return {"h": h,
            "w_words": w_words,
            "w_scales": w_scales,
            "g": g,
            "u_words": u_words,
            "u_scales": u_scales,
            "beta_words": beta_words,
            "beta_scales": beta_scales,
            "c": c}


def softmax_over_tokens(v):
    shifted = v - np.max(v, axis=1, keepdims=True)
    ex = np.exp(shifted)
    return ex / np.sum(ex, axis=1, keepdims=True)


def core(h, w_words, w_scales, g, u_words, u_scales, beta_words, beta_scales, c):
    n_tokens = h.shape[1]
    hq = mxq(f64(h), 2, "e4m3")
    z = f64(g) * np.tanh(hq @ unpack_weight(w_words, w_scales, "e4m3"))
    scores = mxq(z, 2, "e4m3") @ unpack_weight(u_words, u_scales, "e4m3")
    att = softmax_over_tokens(scores)
    p = hq @ unpack_weight(beta_words, beta_scales, "e4m3")
    return n_tokens * att * p + f64(c)


def reference(h, w_words, w_scales, g, u_words, u_scales, beta_words, beta_scales, c):
    R_out = core(h, w_words, w_scales, g, u_words, u_scales, beta_words, beta_scales, c)
    words, scales = planes(np.moveaxis(R_out, 1, 0).reshape(512, -1))
    return R_out, words, scales

from contextlib import ExitStack

import concourse.mybir as mybir
from concourse.masks import make_identity

B, T, D, A, L = 4, 512, 512, 512, 1024
P = 128
NT = T // P
NL = L // P

F32 = mybir.dt.float32
BF16 = mybir.dt.bfloat16
I32 = mybir.dt.int32
U8 = mybir.dt.uint8
FP8X4 = mybir.dt.float8_e4m3fn_x4
ACT = mybir.ActivationFunctionType
ALU = mybir.AluOpType
AX = mybir.AxisListType

PB = {"s": 3, "p": 2, "t": 2, "z": 1}
FLOPS = 2 * B * T * (D * A + A * L + D * L)


def tile_laatlabelwisetokenevidence_x2_kernel(
    tc, h, w_words, w_scales, g, u_words, u_scales, beta_words, beta_scales, c, out_0, out_1, out_2
):
    nc = tc.nc
    out_words = out_1[0].rearrange("p m t -> p (m t)")

    with ExitStack() as ctx:
        const = ctx.enter_context(tc.tile_pool(name="const", bufs=1))
        stage = ctx.enter_context(tc.tile_pool(name="stage", bufs=4))
        keep = ctx.enter_context(tc.tile_pool(name="keep", bufs=2))
        stats = ctx.enter_context(tc.tile_pool(name="stats", bufs=4))
        psum = ctx.enter_context(tc.psum_pool(name="psum", bufs=2))
        ctx.enter_context(tc.manual_schedule())

        h_sb = {}
        for b in range(B):
            for hf in range(2):
                h_sb[b, hf] = const.tile([P, 2, D], BF16, name="h_sb_%d_%d" % (b, hf), align_bytes=64)

        def load_h(b, hf):
            src = h[b].rearrange("(p t) d -> p t d", t=NT)
            nc.sync.dma_start(out=h_sb[b, hf][:], in_=src[:, 2 * hf : 2 * hf + 2, :])

        warm = const.tile([P, 1], F32, name="warm")
        nc.vector.memset(warm[:], 0.0)
        w_raw = const.tile([P, A], I32, name="w_raw", align_bytes=64)
        ws_raw = const.tile([P, A], U8, name="ws_raw", align_bytes=64)
        u_sb = const.tile([P, L], I32, name="u_sb", align_bytes=64)
        us_sb = const.tile([P, L], U8, name="us_sb", align_bytes=64)
        b_sb = const.tile([P, L], I32, name="b_sb", align_bytes=64)
        bs_sb = const.tile([P, L], U8, name="bs_sb", align_bytes=64)
        g_bf = const.tile([P, 4], BF16, name="g_bf")
        c_rows = const.tile([P, P], BF16, name="c_rows", align_bytes=64)
        nc.vector.memset(ws_raw[:].bitcast(I32), 0)
        nc.vector.memset(us_sb[:].bitcast(I32), 0)
        nc.vector.memset(bs_sb[:].bitcast(I32), 0)
        nc.vector.memset(c_rows[:], 0.0)

        load_h(0, 0)
        nc.sync.dma_start(out=w_raw[:], in_=w_words[0].rearrange("p n t -> p (n t)").bitcast(I32))
        load_h(0, 1)
        for r in range(4):
            nc.scalar.dma_start(out=ws_raw[r:P:32, :].bitcast(I32), in_=w_scales[0, r:16:4, :].bitcast(I32))
        nc.scalar.dma_start(out=g_bf[:], in_=g.rearrange("(p t) -> p t", t=4))
        nc.scalar.dma_start(out=c_rows[0:NL, :], in_=c.rearrange("(j p) -> j p", p=P))
        nc.sync.dma_start(out=u_sb[:], in_=u_words[0].rearrange("p n t -> p (n t)").bitcast(I32))
        for r in range(4):
            nc.sync.dma_start(out=us_sb[r:P:32, :].bitcast(I32), in_=u_scales[0, r:16:4, :].bitcast(I32))
        nc.sync.dma_start(out=b_sb[:], in_=beta_words[0].rearrange("p n t -> p (n t)").bitcast(I32))
        for r in range(4):
            nc.sync.dma_start(out=bs_sb[r:P:32, :].bitcast(I32), in_=beta_scales[0, r:16:4, :].bitcast(I32))
        for b in range(1, B):
            load_h(b, 0)
            load_h(b, 1)

        nc.scalar.activation(out=warm[:], in_=warm[:], func=ACT.Exp)
        ident = const.tile([P, P], F32, name="ident", align_bytes=64)
        make_identity(nc, ident[:])
        w_sb = const.tile([P, 4, P], I32, name="w_sb", align_bytes=64)
        ws_sb = const.tile([P, 4, P], U8, name="ws_sb", align_bytes=64)
        g_sb = const.tile([P, 4], F32, name="g_sb")
        c_f32 = const.tile([P, P], F32, name="c_f32", align_bytes=64)
        c_sb = const.tile([P, NL], F32, name="c_sb")

        def prep_w():
            nc.vector.tensor_copy(out=w_sb[:], in_=w_raw[:].rearrange("p (m t) -> p t m", t=4))
            nc.vector.tensor_copy(out=ws_sb[:], in_=ws_raw[:].rearrange("p (m t) -> p t m", t=4))
            nc.vector.tensor_copy(out=g_sb[:], in_=g_bf[:])

        def prep_c():
            nc.vector.tensor_copy(out=c_f32[:], in_=c_rows[:])
            ct = psum.tile([P, P], F32, name="ct", tag="t", bufs=PB["t"])
            nc.tensor.transpose(ct[:], c_f32[:], ident[:])
            nc.vector.tensor_copy(out=c_sb[:], in_=ct[:, 0:NL])

        h_codes, h_scales, z_codes, z_scales, z_t, z_b = {}, {}, {}, {}, {}, {}
        hg = {}

        def h_turn(b, i, tag):
            if i == 0:
                h_codes[b] = keep.tile([P, T], I32, name="h_codes", tag="h_codes", align_bytes=64)
                h_scales[b] = keep.tile([P, T], U8, name="h_scales", tag="h_scales", align_bytes=64)
            words = h_sb[b, i // 2][:].bitcast(F32)
            bank = psum.tile([P, 2, P], F32, name="ht", tag=tag, bufs=PB[tag])
            for e in range(2):
                nc.tensor.transpose(bank[:, e, :], words[:, i % 2, e : D // 2 : 2], ident[:])
            hg[b, i] = stage.tile([P, P, 4], BF16, name="hg", tag="hg", align_bytes=64)
            nc.scalar.copy(out=hg[b, i][:].bitcast(F32), in_=bank[:].rearrange("m e p -> m p e"))

        def h_quant(b, i):
            cols = slice(P * i, P * (i + 1))
            nc.vector.quantize_mx(
                out=h_codes[b][:, cols].bitcast(FP8X4),
                scales=h_scales[b][:, cols],
                in_=hg[b, i][:].rearrange("m p t -> m (p t)"),
            )

        def z_mm(b, i, tag):
            cols = slice(P * i, P * (i + 1))
            bank = psum.tile([P, 4, P], F32, name="zp", tag=tag, bufs=PB[tag])
            for t in range(4):
                nc.tensor.matmul_mx(
                    out=bank[:, t, :],
                    lhsT=w_sb[:, t, :].bitcast(FP8X4),
                    lhsT_scale=ws_sb[:, t, :],
                    rhs=h_codes[b][:, cols].bitcast(FP8X4),
                    rhs_scale=h_scales[b][:, cols],
                    start=True,
                    stop=True,
                )
            z_t[b, i] = stage.tile([P, P, 4], F32, name="z_t", tag="z_t")
            nc.scalar.activation(out=z_t[b, i][:], in_=bank[:].rearrange("m t n -> m n t"), func=ACT.Tanh)

        def z_gain(b, i, eng):
            z_b[b, i] = stage.tile([P, P, 4], BF16, name="z_b", tag="z_b", align_bytes=64)
            eng.tensor_tensor(
                out=z_b[b, i][:],
                in0=z_t[b, i][:],
                in1=g_sb[:].unsqueeze(1).to_broadcast([P, P, 4]),
                op=ALU.mult,
            )

        def z_quant(b, i):
            if i == 0:
                z_codes[b] = keep.tile([P, T], I32, name="z_codes", tag="z_codes", align_bytes=64)
                z_scales[b] = keep.tile([P, T], U8, name="z_scales", tag="z_scales", align_bytes=64)
            cols = slice(P * i, P * (i + 1))
            nc.vector.quantize_mx(
                out=z_codes[b][:, cols].bitcast(FP8X4),
                scales=z_scales[b][:, cols],
                in_=z_b[b, i][:].rearrange("m p t -> m (p t)"),
            )

        NU = B * NL
        s_ps, p_ps, neg, dsum, rinv, ex, vt, wt = {}, {}, {}, {}, {}, {}, {}, {}
        groups = [list(range(4 * q, 4 * q + 4)) for q in range(NU // 4 - 1)]
        groups += [[NU - 4, NU - 3], [NU - 2], [NU - 1]]
        group_of = {}
        for gi in range(len(groups)):
            for u in groups[gi]:
                group_of[u] = gi
        y32, y16 = {}, {}
        o_scales = const.tile([P, B * L], U8, name="o_scales", align_bytes=64)

        def s_mm(u):
            b, j = divmod(u, NL)
            cols = slice(P * j, P * (j + 1))
            s_ps[u] = psum.tile([P, T], F32, name="s_ps", tag="s", bufs=PB["s"])
            nc.tensor.matmul_mx(
                out=s_ps[u][:],
                lhsT=u_sb[:, cols].bitcast(FP8X4),
                lhsT_scale=us_sb[:, cols],
                rhs=z_codes[b][:].bitcast(FP8X4),
                rhs_scale=z_scales[b][:],
                start=True,
                stop=True,
            )

        def p_mm(u):
            b, j = divmod(u, NL)
            cols = slice(P * j, P * (j + 1))
            p_ps[u] = psum.tile([P, T], F32, name="p_ps", tag="p", bufs=PB["p"])
            nc.tensor.matmul_mx(
                out=p_ps[u][:],
                lhsT=b_sb[:, cols].bitcast(FP8X4),
                lhsT_scale=bs_sb[:, cols],
                rhs=h_codes[b][:].bitcast(FP8X4),
                rhs_scale=h_scales[b][:],
                start=True,
                stop=True,
            )

        def vmax(u):
            neg[u] = stats.tile([P, 1], F32, name="neg", tag="neg")
            nc.vector.tensor_reduce(out=neg[u][:], in_=s_ps[u][:], axis=AX.X, op=ALU.max, negate=True)

        def sexp(u):
            ex[u] = stage.tile([P, T], F32, name="ex", tag="ex")
            dsum[u] = stats.tile([P, 1], F32, name="dsum", tag="dsum")
            nc.scalar.activation(
                out=ex[u][:], in_=s_ps[u][:], func=ACT.Exp, bias=neg[u][:], accum_out=dsum[u][:]
            )

        def vmul(u):
            rinv[u] = stats.tile([P, 1], F32, name="rinv", tag="rinv")
            nc.vector.reciprocal(out=rinv[u][:], in_=dsum[u][:])
            vt[u] = stage.tile([P, T], F32, name="vt", tag="vt")
            nc.vector.scalar_tensor_tensor(
                out=vt[u][:], in0=p_ps[u][:], scalar=float(T), in1=ex[u][:], op0=ALU.mult, op1=ALU.mult
            )

        def affine(u):
            wt[u] = stage.tile([P, T], F32, name="wt", tag="wt")
            j = u % NL
            nc.gpsimd.tensor_scalar(
                out=wt[u][:], in0=vt[u][:], scalar1=rinv[u][:], scalar2=c_sb[:, j : j + 1], op0=ALU.mult, op1=ALU.add
            )

        def turn(u):
            gi = group_of[u]
            n = len(groups[gi])
            k = u - groups[gi][0]
            if k == 0:
                y32[gi] = stage.tile([P, 4, n * P], F32, name="y32", tag="y32")
                y16[gi] = stage.tile([P, n * P, 4], BF16, name="y16", tag="y16", align_bytes=64)
            bank = psum.tile([P, 4, P], F32, name="tp", tag="t", bufs=PB["t"])
            for t in range(4):
                nc.tensor.transpose(bank[:, t, :], wt[u][:, P * t : P * (t + 1)], ident[:])
            nc.scalar.copy(out=y32[gi][:, :, P * k : P * (k + 1)], in_=bank[:])

        def round_out(u):
            gi = group_of[u]
            k = u - groups[gi][0]
            cols = slice(P * k, P * (k + 1))
            nc.vector.tensor_copy(out=y16[gi][:, cols, :], in_=y32[gi][:, :, cols].rearrange("p t l -> p l t"))

        def store_y(gi):
            u0, n = groups[gi][0], len(groups[gi])
            b, j = divmod(u0, NL)
            dst = out_0[b].rearrange("(p t) l -> p t l", t=4)
            nc.sync.dma_start(out=dst[:, :, P * j : P * (j + n)], in_=y32[gi][:])

        def quant_out(gi):
            u0, n = groups[gi][0], len(groups[gi])
            m0, m1 = P * u0, P * (u0 + n)
            o_codes = stage.tile([P, n * P], I32, name="o_codes", tag="o_codes", align_bytes=64)
            nc.vector.quantize_mx(
                out=o_codes[:].bitcast(FP8X4),
                scales=o_scales[:, m0:m1],
                in_=y16[gi][:].rearrange("p l t -> p (l t)"),
            )
            nc.sync.dma_start(out=out_words[:, 4 * m0 : 4 * m1].bitcast(I32), in_=o_codes[:])
            u1 = u0 + n
            if u1 % NL == 0:
                m0 = P * (u1 - NL)
                for q in range(4):
                    nc.sync.dma_start(
                        out=out_2[0, 4 * q : 4 * q + 4, m0:m1].bitcast(I32),
                        in_=o_scales[32 * q : 32 * q + 4, m0:m1].bitcast(I32),
                    )

        h_turn(0, 0, "t")
        h_turn(0, 1, "t")
        prep_w()
        h_quant(0, 0)
        z_mm(0, 0, "z")
        h_quant(0, 1)
        z_mm(0, 1, "s")
        h_turn(0, 2, "t")
        z_gain(0, 0, nc.vector)
        h_quant(0, 2)
        z_mm(0, 2, "s")
        z_quant(0, 0)
        h_turn(0, 3, "t")
        z_gain(0, 1, nc.vector)
        h_quant(0, 3)
        z_mm(0, 3, "s")
        z_quant(0, 1)
        prep_c()
        z_gain(0, 2, nc.vector)
        z_gain(0, 3, nc.vector)
        z_quant(0, 2)
        z_quant(0, 3)
        s_mm(0)
        s_mm(1)
        p_mm(0)
        vmax(0)
        sexp(0)

        for k in range(NU + 5):
            b, j = divmod(k, NL)
            nb = b + 1
            if k + 1 < NU:
                vmax(k + 1)
            if 0 <= k - 2 < NU:
                turn(k - 2)
            if k + 2 < NU:
                s_mm(k + 2)
            if k + 1 < NU:
                p_mm(k + 1)
            if nb < B:
                if 0 <= j - 1 < 4:
                    z_mm(nb, j - 1, "z")
                if j < 4:
                    h_turn(nb, j, "t")
                if 0 <= j - 2 < 4:
                    z_gain(nb, j - 2, nc.gpsimd)
            if k + 1 < NU:
                sexp(k + 1)
            if k < NU:
                vmul(k)
                affine(k)
            if 0 <= k - 3 < NU:
                round_out(k - 3)
                gi = group_of[k - 3]
                if groups[gi][-1] == k - 3:
                    store_y(gi)
            if nb < B:
                if j < 4:
                    h_quant(nb, j)
                if 0 <= j - 2 < 4:
                    z_quant(nb, j - 2)
            if 0 <= k - 4 < NU:
                gi = group_of[k - 4]
                if groups[gi][-1] == k - 4:
                    quant_out(gi)
